import numpy as np
import ml_dtypes


def mxq(x, axis, fmt="e4m3"):
    dtype, down = {"e4m3": (ml_dtypes.float8_e4m3fn, 7), "e5m2": (ml_dtypes.float8_e5m2, 14)}[fmt]
    v = np.moveaxis(np.asarray(x, np.float32).astype(ml_dtypes.bfloat16).astype(np.float64), axis, -1)
    blocks = v.reshape(v.shape[:-1] + (-1, 32))
    amax = np.abs(blocks).max(-1, keepdims=True)
    byte = np.maximum(np.where(amax > 0, np.frexp(amax)[1] - 1 + 127, 0) - down, 1)
    scale = np.exp2(byte - 127.0)
    codes = (blocks / scale).astype(np.float32).astype(dtype).astype(np.float64)
    return np.moveaxis((codes * scale).reshape(v.shape), -1, axis)


WIDE = False


def mx_kscale(k):
    if not WIDE:
        return np.ones(k)
    levels = np.array([10, -10, 5, -5, 0])
    if k % 512:
        return np.exp2(np.random.permutation(np.resize(levels, k // 32))).repeat(32)
    a = np.empty((k // 512, 16))
    for p in range(k // 512):
        a[p, :8] = np.random.permutation(np.resize(levels, 8))
        for g in range(8):
            far = levels[np.abs(levels - a[p, g]) >= 10]
            a[p, g + 8] = far[np.random.randint(len(far))]
    return np.exp2(a.ravel()).repeat(32)


def f64(x):
    return np.asarray(x).astype(np.float64)


def striped(idx):
    return np.tile(np.asarray(idx).reshape(-1, 16).T, (8, 1)).astype(np.uint16)


def unstriped(offs):
    return offs[:16].T.reshape(-1).astype(np.int64)


E2M1 = np.array([0.0, 0.5, 1.0, 1.5, 2.0, 3.0, 4.0, 6.0, -0.0, -0.5, -1.0, -1.5, -2.0, -3.0, -4.0, -6.0])


def pack_weight(w, fmt):
    k, n = w.shape
    w = f64(np.asarray(w, np.float32).astype(ml_dtypes.bfloat16)).reshape(k // 32, 32, n)
    amax = np.abs(w).max(1)
    if fmt == "e4m3":
        byte = np.frexp(amax)[1] - 1 + 127 - 7
    else:
        mant, ex = np.frexp(amax / 6.0)
        byte = np.where(mant > 0.5, ex, ex - 1) + 127
    byte = np.clip(np.where(amax > 0, byte, 1), 1, 254)
    scaled = (w * np.exp2(127.0 - byte)[:, None, :]).reshape(k, n).astype(np.float32)
    by_word = np.ascontiguousarray(scaled.reshape(k // 512, 128, 4, n).transpose(0, 1, 3, 2))
    if fmt == "e4m3":
        words = by_word.astype(ml_dtypes.float8_e4m3fn).view(np.uint8)
    else:
        c = by_word.astype(ml_dtypes.float4_e2m1fn).view(np.uint8) & 0xF
        words = (c[..., 0::2] | (c[..., 1::2] << 4)).reshape(k // 512, 128, 2 * n)
    return np.ascontiguousarray(words), np.ascontiguousarray(byte.astype(np.uint8).reshape(k // 512, 16, n))


def unpack_weight(words, scales, fmt):
    g, _, n = scales.shape
    words = np.ascontiguousarray(words).reshape(g, 128, n, -1)
    if fmt == "e4m3":
        vals = words.view(ml_dtypes.float8_e4m3fn).astype(np.float64)
    else:
        nib = np.empty((g, 128, n, 4), np.uint8)
        nib[..., 0::2] = words & 0xF
        nib[..., 1::2] = words >> 4
        vals = E2M1[nib]
    vals = vals * np.repeat(np.exp2(scales.astype(np.float64) - 127.0), 8, axis=1)[..., None]
    return vals.transpose(0, 1, 3, 2).reshape(g * 512, n)


B, N, T, D, DV, NQ = 1, 512, 1024, 512, 128, 256
CAP = 2.0


def setup_inputs():
    n = np.random.standard_normal
    idx = np.sort(np.random.permutation(T)[:B * N].reshape(B, N), axis=1).reshape(-1)
    s = mx_kscale(D)[:, None]
    u = np.ones(T)
    u[idx] = mx_kscale(B * N)
    r = np.random.uniform(0.5, 2.0, T)
    k = n((D, T)) / s
    v = n((DV, T)) / (u * r)
    kp = pack_weight(k, "e4m3")
    return {
        "qT": (n((B, D, NQ)) * s * (0.80 / np.sqrt(D))).astype(np.float32),
        "k_words": kp[0],
        "k_scales": kp[1],
        "vT": v.astype(np.float32),
        "vs": np.tile(u * r, (128, 1)).astype(np.float32),
        "og": n((B, NQ, DV)).astype(np.float32),
        "offs": striped(idx),
    }


def reference(qT, k_words, k_scales, vT, vs, og, offs):
    idx = unstriped(offs)
    k = unpack_weight(k_words, k_scales, "e4m3")
    v = f64(vT)
    pick = lambda x: x[:, idx].reshape(x.shape[0], B, N).transpose(1, 0, 2)
    q = f64(qT)
    score = mxq(q, 1, "e4m3").transpose(0, 2, 1) @ pick(k)
    score = CAP * np.tanh(score / CAP)
    m = score.max(-1, keepdims=True)
    p = np.exp(score - m)
    total = p.sum(-1, keepdims=True)
    w = p * pick(f64(vs))[:, :1, :]
    y = mxq(w, 2, "e4m3") @ mxq(pick(v).transpose(0, 2, 1), 1, "e4m3")
    y = y / total
    y = y / (1.0 + np.exp(-f64(og)))
    return y

@@ -1,0 +1,149 @@
+from contextlib import ExitStack
+
+import concourse.mybir as mybir
+
+N, T, D, DV, NQ = 512, 1024, 512, 128, 256
+CAP = 2.0
+FLOPS = 2 * NQ * N * D + 2 * NQ * N * DV
+
+F32 = mybir.dt.float32
+BF16 = mybir.dt.bfloat16
+I32 = mybir.dt.int32
+U32 = mybir.dt.uint32
+U16 = mybir.dt.uint16
+U8 = mybir.dt.uint8
+FP8X4 = mybir.dt.float8_e4m3fn_x4
+ACT = mybir.ActivationFunctionType
+ALU = mybir.AluOpType
+
+P = 128
+PACK = 4
+QT = NQ // P
+VS_ROW = 96
+
+
+def tile_attend_soft_cap_gate_srtq256n512t1024_kernel(tc, qT, k_words, k_scales, vT, vs, og, offs, out):
+    nc = tc.nc
+    with ExitStack() as ctx:
+        sb = ctx.enter_context(tc.tile_pool(name="sb", bufs=1))
+        ps = ctx.enter_context(tc.psum_pool(name="ps", bufs=1))
+
+        def tile(name, shape, dtype, tag=None):
+            return sb.tile(shape, dtype, name=name, tag=tag or name, align_bytes=64)
+
+        offsets = sb.tile([P, N // 16], U16, name="offsets")
+        nc.sync.dma_start(offsets[:], offs)
+
+        vs_pool = tile("vs_pool", [P, T], F32)
+        nc.sync.dma_start(vs_pool[VS_ROW:P, :], vs[VS_ROW:P, :])
+        q_raw = tile("q_raw", [P, PACK, NQ], F32)
+        nc.sync.dma_start(q_raw[:], qT[0].rearrange("(p j) q -> p j q", j=PACK))
+        ks_pool = tile("ks_pool", [P, T], U8)
+        nc.vector.memset(ks_pool[:].bitcast(I32), 0)
+        for r in range(4):
+            (nc.scalar if r % 2 else nc.sync).dma_start(ks_pool[r:P:32, :].bitcast(I32), k_scales[0, r:16:4, :].bitcast(I32))
+        nc.vector.memset(vs_pool[0:VS_ROW, :].bitcast(I32), 0)
+
+        ident = tile("ident", [P, P], F32)
+        for h in range(2):
+            zeros = tile(f"zeros{h}", [P, P // 2], F32)
+            nc.gpsimd.memset(zeros[:], 0.0)
+            nc.gpsimd.affine_select(out=ident[:, h * (P // 2) : (h + 1) * (P // 2)], in_=zeros[:],
+                                    compare_op=ALU.not_equal, fill=1.0, base=-h * (P // 2),
+                                    pattern=[[-1, P // 2]], channel_multiplier=1)
+
+        kw_pool = tile("kw_pool", [P, T], I32, tag="zeros0")
+        nc.sync.dma_start(kw_pool[:], k_words[0].rearrange("p n t -> p (n t)").bitcast(I32))
+        v_pool = tile("v_pool", [P, T], F32, tag="zeros1")
+        nc.sync.dma_start(v_pool[:], vT)
+
+        vs_g = tile("vs_g", [P, N], F32)
+        nc.vector.tensor_copy(vs_g[:], vs_pool[:].indirect(offsets[:]))
+        ks_g = tile("ks_g", [P, N], U8)
+        nc.vector.tensor_copy(ks_g[:], ks_pool[:].indirect(offsets[:]))
+
+        q_codes, q_scales = [], []
+        q_bf = []
+        for i in range(QT):
+            q_bf.append(tile(f"q_bf{i}", [P, P, PACK], BF16))
+            nc.scalar.activation(q_bf[i][:], q_raw[:, :, i * P : (i + 1) * P].rearrange("p j q -> p q j"), ACT.Copy)
+            q_codes.append(tile(f"q_codes{i}", [P, P], U32))
+            q_scales.append(tile(f"q_scales{i}", [P, P], U8))
+
+        def quantise(codes, scales, grouped):
+            nc.vector.quantize_mx(codes[:].bitcast(FP8X4), scales[:], grouped[:].rearrange("p c j -> p (c j)"))
+
+        quantise(q_codes[0], q_scales[0], q_bf[0])
+        kw_g = tile("kw_g", [P, N], U32)
+        nc.vector.tensor_copy(kw_g[:], kw_pool[:].bitcast(U32).indirect(offsets[:]))
+        quantise(q_codes[1], q_scales[1], q_bf[1])
+        og_sb = tile("og_sb", [P, QT, DV], F32, tag="zeros0")
+        nc.sync.dma_start(og_sb[:], og[0].rearrange("(i p) e -> p i e", p=P))
+
+        vs_t = ps.tile([P, PACK, P], F32, name="vs_t")
+        for t in range(PACK):
+            nc.tensor.transpose(vs_t[:, t, :], vs_g[:, t:N:PACK], ident[:])
+        vs_col = tile("vs_col", [P, PACK], F32)
+        nc.scalar.copy(vs_col[:], vs_t[:, :, VS_ROW])
+
+        th = []
+        for i in range(QT):
+            score = ps.tile([P, N], F32, name=f"score{i}")
+            nc.tensor.matmul_mx(score[:], lhsT=q_codes[i][:].bitcast(FP8X4), lhsT_scale=q_scales[i][:],
+                                rhs=kw_g[:].bitcast(FP8X4), rhs_scale=ks_g[:], start=True, stop=True)
+            th.append(tile(f"th{i}", [P, PACK, P], F32))
+            nc.scalar.activation(th[i][:], score[:].rearrange("p (s t) -> p t s", t=PACK), ACT.Tanh, scale=1.0 / CAP)
+
+        v_g = tile("v_g", [P, N], BF16)
+        nc.vector.tensor_copy(v_g[:], v_pool[:].indirect(offsets[:]))
+
+        total = tile("total", [P, QT], F32)
+        p = []
+        for i in range(QT):
+            neg_c = tile(f"neg_c{i}", [P, N], F32)
+            neg_m = tile(f"neg_m{i}", [P, 1], F32)
+            nc.vector.tensor_scalar(neg_c[:], th[i][:].rearrange("p t s -> p (t s)"), -CAP, None, ALU.mult, ALU.min,
+                                    accum_out=neg_m[:])
+            p.append(tile(f"p{i}", [P, N], F32))
+            nc.scalar.activation(p[i][:], neg_c[:], ACT.Exp, bias=neg_m[:], scale=-1.0, accum_out=total[:, i : i + 1])
+
+        v_t = ps.tile([P, 2, DV], F32, name="v_t")
+        v_words = v_g[:].bitcast(F32)
+        for u in range(2):
+            nc.tensor.transpose(v_t[:, u, :], v_words[:, u : N // 2 : 2], ident[:])
+        v_bf = tile("v_bf", [P, DV, PACK], BF16)
+        nc.scalar.copy(v_bf[:].bitcast(F32), v_t[:].rearrange("p u e -> p e u"))
+        v_codes = tile("v_codes", [P, DV], U32)
+        v_scales = tile("v_scales", [P, DV], U8)
+        quantise(v_codes, v_scales, v_bf)
+
+        w_bf = []
+        for i in range(QT):
+            p_t = ps.tile([P, PACK, P], F32, name=f"p_t{i}")
+            for t in range(PACK):
+                nc.tensor.transpose(p_t[:, t, :], p[i][:, t * P : (t + 1) * P], ident[:])
+            w_bf.append(tile(f"w_bf{i}", [P, P, PACK], BF16))
+            nc.vector.tensor_tensor(w_bf[i][:], p_t[:].rearrange("p t q -> p q t"),
+                                    vs_col[:].unsqueeze(1).to_broadcast([P, P, PACK]), ALU.mult)
+
+        gate_th = tile("gate_th", [P, QT, DV], F32, tag="neg_c1")
+        nc.scalar.activation(gate_th[:], og_sb[:], ACT.Tanh, scale=0.5)
+        gate = tile("gate", [P, QT, DV], F32)
+        nc.scalar.activation(gate[:], gate_th[:], ACT.Copy, scale=0.5, bias=0.5)
+
+        ys = []
+        for i in range(QT):
+            w_codes = tile(f"w_codes{i}", [P, P], U32)
+            w_scales = tile(f"w_scales{i}", [P, P], U8)
+            quantise(w_codes, w_scales, w_bf[i])
+            ys.append(ps.tile([P, DV], F32, name=f"y{i}"))
+            nc.tensor.matmul_mx(ys[i][:], lhsT=w_codes[:].bitcast(FP8X4), lhsT_scale=w_scales[:],
+                                rhs=v_codes[:].bitcast(FP8X4), rhs_scale=v_scales[:], start=True, stop=True)
+
+        inv = tile("inv", [P, QT], F32)
+        nc.vector.reciprocal(inv[:], total[:])
+        for i in range(QT):
+            res = tile(f"res{i}", [P, DV], F32)
+            nc.vector.scalar_tensor_tensor(res[:], ys[i][:], inv[:, i : i + 1], gate[:, i, :], ALU.mult, ALU.mult)
+            queue = nc.sync if i == QT - 1 else nc.scalar
+            queue.dma_start(out[0, i * P : (i + 1) * P, :], res[:])

@@ -1,6 +1,7 @@
 from contextlib import ExitStack
 
 import concourse.mybir as mybir
+from concourse.masks import make_identity
 
 N, T, D, DV, NQ = 512, 1024, 512, 128, 256
 CAP = 2.0
@@ -19,7 +20,8 @@ ALU = mybir.AluOpType
 P = 128
 PACK = 4
 QT = NQ // P
-VS_ROW = 96
+H = N // 2
+PREFIX = T - (N - H)
 
 
 def tile_attend_soft_cap_gate_srtq256n512t1024_kernel(tc, qT, k_words, k_scales, vT, vs, og, offs, out):
@@ -31,73 +33,67 @@ def tile_attend_soft_cap_gate_srtq256n512t1024_kernel(tc, qT, k_words, k_scales,
         def tile(name, shape, dtype, tag=None):
             return sb.tile(shape, dtype, name=name, tag=tag or name, align_bytes=64)
 
+        def quantise(codes, scales, grouped):
+            nc.vector.quantize_mx(codes.bitcast(FP8X4), scales, grouped.rearrange("p c j -> p (c j)"))
+
         offsets = sb.tile([P, N // 16], U16, name="offsets")
         nc.sync.dma_start(offsets[:], offs)
-
-        vs_pool = tile("vs_pool", [P, T], F32)
-        nc.sync.dma_start(vs_pool[VS_ROW:P, :], vs[VS_ROW:P, :])
-        q_raw = tile("q_raw", [P, PACK, NQ], F32)
-        nc.sync.dma_start(q_raw[:], qT[0].rearrange("(p j) q -> p j q", j=PACK))
+        kw_pool = tile("kw_pool", [P, T], I32)
+        kw_rows = k_words[0].rearrange("p n t -> p (n t)").bitcast(I32)
+        nc.sync.dma_start(kw_pool[:, 0:PREFIX], kw_rows[:, 0:PREFIX])
         ks_pool = tile("ks_pool", [P, T], U8)
         nc.vector.memset(ks_pool[:].bitcast(I32), 0)
         for r in range(4):
             (nc.scalar if r % 2 else nc.sync).dma_start(ks_pool[r:P:32, :].bitcast(I32), k_scales[0, r:16:4, :].bitcast(I32))
-        nc.vector.memset(vs_pool[0:VS_ROW, :].bitcast(I32), 0)
+        vs_pool = tile("vs_pool", [P, T], F32)
+        nc.vector.memset(vs_pool[:].bitcast(I32), 0)
+        q_rows = qT[0].rearrange("(p j) q -> p j q", j=PACK)
+        q_raw = [tile(f"q_raw{i}", [P, PACK, P], F32) for i in range(QT)]
+        nc.sync.dma_start(q_raw[0][:], q_rows[:, :, 0:P])
+        nc.sync.dma_start(kw_pool[:, PREFIX:T], kw_rows[:, PREFIX:T])
+        nc.sync.dma_start(q_raw[1][:], q_rows[:, :, P:NQ])
+        nc.sync.dma_start(vs_pool[0:1, :], vs[0:1, :])
+        v_pool = tile("v_pool", [P, T], F32)
+        nc.sync.dma_start(v_pool[:], vT)
+        og_sb = tile("og_sb", [P, QT, DV], F32)
+        nc.sync.dma_start(og_sb[:], og[0].rearrange("(i p) e -> p i e", p=P))
 
         ident = tile("ident", [P, P], F32)
-        for h in range(2):
-            zeros = tile(f"zeros{h}", [P, P // 2], F32)
-            nc.gpsimd.memset(zeros[:], 0.0)
-            nc.gpsimd.affine_select(out=ident[:, h * (P // 2) : (h + 1) * (P // 2)], in_=zeros[:],
-                                    compare_op=ALU.not_equal, fill=1.0, base=-h * (P // 2),
-                                    pattern=[[-1, P // 2]], channel_multiplier=1)
+        make_identity(nc, ident[:])
 
-        kw_pool = tile("kw_pool", [P, T], I32, tag="zeros0")
-        nc.sync.dma_start(kw_pool[:], k_words[0].rearrange("p n t -> p (n t)").bitcast(I32))
-        v_pool = tile("v_pool", [P, T], F32, tag="zeros1")
-        nc.sync.dma_start(v_pool[:], vT)
-
-        vs_g = tile("vs_g", [P, N], F32)
-        nc.vector.tensor_copy(vs_g[:], vs_pool[:].indirect(offsets[:]))
-        ks_g = tile("ks_g", [P, N], U8)
-        nc.vector.tensor_copy(ks_g[:], ks_pool[:].indirect(offsets[:]))
-
-        q_codes, q_scales = [], []
         q_bf = []
         for i in range(QT):
             q_bf.append(tile(f"q_bf{i}", [P, P, PACK], BF16))
-            nc.scalar.activation(q_bf[i][:], q_raw[:, :, i * P : (i + 1) * P].rearrange("p j q -> p q j"), ACT.Copy)
-            q_codes.append(tile(f"q_codes{i}", [P, P], U32))
-            q_scales.append(tile(f"q_scales{i}", [P, P], U8))
+            nc.scalar.activation(q_bf[i][:], q_raw[i][:].rearrange("p j q -> p q j"), ACT.Copy)
+        q_codes = [tile(f"q_codes{i}", [P, P], U32) for i in range(QT)]
+        q_scales = [tile(f"q_scales{i}", [P, P], U8) for i in range(QT)]
 
-        def quantise(codes, scales, grouped):
-            nc.vector.quantize_mx(codes[:].bitcast(FP8X4), scales[:], grouped[:].rearrange("p c j -> p (c j)"))
-
-        quantise(q_codes[0], q_scales[0], q_bf[0])
-        kw_g = tile("kw_g", [P, N], U32)
-        nc.vector.tensor_copy(kw_g[:], kw_pool[:].bitcast(U32).indirect(offsets[:]))
-        quantise(q_codes[1], q_scales[1], q_bf[1])
-        og_sb = tile("og_sb", [P, QT, DV], F32, tag="zeros0")
-        nc.sync.dma_start(og_sb[:], og[0].rearrange("(i p) e -> p i e", p=P))
-
-        vs_t = ps.tile([P, PACK, P], F32, name="vs_t")
-        for t in range(PACK):
-            nc.tensor.transpose(vs_t[:, t, :], vs_g[:, t:N:PACK], ident[:])
-        vs_col = tile("vs_col", [P, PACK], F32)
-        nc.scalar.copy(vs_col[:], vs_t[:, :, VS_ROW])
+        kw_g = [tile("kw_g0", [P, H], U32), tile("kw_g1", [P, H], U32, tag="q_raw0")]
+        nc.vector.tensor_copy(kw_g[0][:], kw_pool[:, 0:PREFIX].bitcast(U32).indirect(offsets[:, 0 : H // 16]))
+        ks_g = tile("ks_g", [P, N], U8)
+        nc.vector.tensor_copy(ks_g[:], ks_pool[:].indirect(offsets[:]))
+        quantise(q_codes[0][:], q_scales[0][:], q_bf[0][:])
+        nc.vector.tensor_copy(kw_g[1][:], kw_pool[:].bitcast(U32).indirect(offsets[:, H // 16 : N // 16]))
+        quantise(q_codes[1][:], q_scales[1][:], q_bf[1][:])
+        vs_g = tile("vs_g", [P, N], F32, tag="q_raw1")
+        nc.vector.tensor_copy(vs_g[:], vs_pool[:].indirect(offsets[:]))
 
         th = []
         for i in range(QT):
             score = ps.tile([P, N], F32, name=f"score{i}")
-            nc.tensor.matmul_mx(score[:], lhsT=q_codes[i][:].bitcast(FP8X4), lhsT_scale=q_scales[i][:],
-                                rhs=kw_g[:].bitcast(FP8X4), rhs_scale=ks_g[:], start=True, stop=True)
+            for h in range(2):
+                cols = slice(h * H, (h + 1) * H)
+                nc.tensor.matmul_mx(score[:, cols], lhsT=q_codes[i][:].bitcast(FP8X4), lhsT_scale=q_scales[i][:],
+                                    rhs=kw_g[h][:].bitcast(FP8X4), rhs_scale=ks_g[:, cols], start=True, stop=True)
             th.append(tile(f"th{i}", [P, PACK, P], F32))
             nc.scalar.activation(th[i][:], score[:].rearrange("p (s t) -> p t s", t=PACK), ACT.Tanh, scale=1.0 / CAP)
 
-        v_g = tile("v_g", [P, N], BF16)
-        nc.vector.tensor_copy(v_g[:], v_pool[:].indirect(offsets[:]))
+        vs_t = ps.tile([P, PACK, P], F32, name="vs_t")
+        for t in range(PACK):
+            nc.tensor.transpose(vs_t[:, t, :], vs_g[:, t:N:PACK], ident[:])
 
         total = tile("total", [P, QT], F32)
+        parts = tile("parts", [P, 2], F32)
         p = []
         for i in range(QT):
             neg_c = tile(f"neg_c{i}", [P, N], F32)
@@ -105,17 +101,19 @@ def tile_attend_soft_cap_gate_srtq256n512t1024_kernel(tc, qT, k_words, k_scales,
             nc.vector.tensor_scalar(neg_c[:], th[i][:].rearrange("p t s -> p (t s)"), -CAP, None, ALU.mult, ALU.min,
                                     accum_out=neg_m[:])
             p.append(tile(f"p{i}", [P, N], F32))
-            nc.scalar.activation(p[i][:], neg_c[:], ACT.Exp, bias=neg_m[:], scale=-1.0, accum_out=total[:, i : i + 1])
+            if i == 0:
+                nc.scalar.activation(p[i][:], neg_c[:], ACT.Exp, bias=neg_m[:], scale=-1.0, accum_out=total[:, 0:1])
+            else:
+                for h in range(2):
+                    cols = slice(h * H, (h + 1) * H)
+                    nc.scalar.activation(p[i][:, cols], neg_c[:, cols], ACT.Exp, bias=neg_m[:], scale=-1.0,
+                                         accum_out=parts[:, h : h + 1])
+                nc.scalar.activation(total[:, 1:2], parts[:, 0:1], ACT.Identity, bias=parts[:, 1:2])
 
-        v_t = ps.tile([P, 2, DV], F32, name="v_t")
-        v_words = v_g[:].bitcast(F32)
-        for u in range(2):
-            nc.tensor.transpose(v_t[:, u, :], v_words[:, u : N // 2 : 2], ident[:])
-        v_bf = tile("v_bf", [P, DV, PACK], BF16)
-        nc.scalar.copy(v_bf[:].bitcast(F32), v_t[:].rearrange("p u e -> p e u"))
-        v_codes = tile("v_codes", [P, DV], U32)
-        v_scales = tile("v_scales", [P, DV], U8)
-        quantise(v_codes, v_scales, v_bf)
+        v_g = tile("v_g", [P, N], BF16, tag="neg_c0")
+        nc.vector.tensor_copy(v_g[:], v_pool[:].indirect(offsets[:]))
+        vs_col = tile("vs_col", [P, PACK], F32, tag="th1")
+        nc.scalar.copy(vs_col[:], vs_t[:, :, 0])
 
         w_bf = []
         for i in range(QT):
@@ -126,24 +124,33 @@ def tile_attend_soft_cap_gate_srtq256n512t1024_kernel(tc, qT, k_words, k_scales,
             nc.vector.tensor_tensor(w_bf[i][:], p_t[:].rearrange("p t q -> p q t"),
                                     vs_col[:].unsqueeze(1).to_broadcast([P, P, PACK]), ALU.mult)
 
+        v_t = ps.tile([P, 2, DV], F32, name="v_t")
+        v_words = v_g[:].bitcast(F32)
+        for u in range(2):
+            nc.tensor.transpose(v_t[:, u, :], v_words[:, u:H:2], ident[:])
+        v_bf = tile("v_bf", [P, DV, PACK], BF16)
+        nc.scalar.copy(v_bf[:].bitcast(F32), v_t[:].rearrange("p u e -> p e u"))
+
+        v_codes = tile("v_codes", [P, DV], U32)
+        v_scales = tile("v_scales", [P, DV], U8)
+        w_codes = [tile("w_codes0", [P, P], U32, tag="p1"), tile("w_codes1", [P, P], U32)]
+        w_scales = [tile(f"w_scales{i}", [P, P], U8) for i in range(QT)]
+        quantise(w_codes[0][:], w_scales[0][:], w_bf[0][:])
+        quantise(v_codes[:], v_scales[:], v_bf[:])
+        quantise(w_codes[1][:], w_scales[1][:], w_bf[1][:])
+
         gate_th = tile("gate_th", [P, QT, DV], F32, tag="neg_c1")
         nc.scalar.activation(gate_th[:], og_sb[:], ACT.Tanh, scale=0.5)
         gate = tile("gate", [P, QT, DV], F32)
         nc.scalar.activation(gate[:], gate_th[:], ACT.Copy, scale=0.5, bias=0.5)
-
-        ys = []
-        for i in range(QT):
-            w_codes = tile(f"w_codes{i}", [P, P], U32)
-            w_scales = tile(f"w_scales{i}", [P, P], U8)
-            quantise(w_codes, w_scales, w_bf[i])
-            ys.append(ps.tile([P, DV], F32, name=f"y{i}"))
-            nc.tensor.matmul_mx(ys[i][:], lhsT=w_codes[:].bitcast(FP8X4), lhsT_scale=w_scales[:],
-                                rhs=v_codes[:].bitcast(FP8X4), rhs_scale=v_scales[:], start=True, stop=True)
-
         inv = tile("inv", [P, QT], F32)
         nc.vector.reciprocal(inv[:], total[:])
+
         for i in range(QT):
+            cols = slice(i * P, (i + 1) * P)
+            y = ps.tile([P, DV], F32, name=f"y{i}")
+            nc.tensor.matmul_mx(y[:], lhsT=w_codes[i][:].bitcast(FP8X4), lhsT_scale=w_scales[i][:],
+                                rhs=v_codes[:].bitcast(FP8X4), rhs_scale=v_scales[:], start=True, stop=True)
             res = tile(f"res{i}", [P, DV], F32)
-            nc.vector.scalar_tensor_tensor(res[:], ys[i][:], inv[:, i : i + 1], gate[:, i, :], ALU.mult, ALU.mult)
-            queue = nc.sync if i == QT - 1 else nc.scalar
-            queue.dma_start(out[0, i * P : (i + 1) * P, :], res[:])
+            nc.vector.scalar_tensor_tensor(res[:], y[:], inv[:, i : i + 1], gate[:, i, :], ALU.mult, ALU.mult)
+            (nc.sync if i == QT - 1 else nc.scalar).dma_start(out[0, cols, :], res[:])

@@ -50,8 +50,8 @@ def tile_attend_soft_cap_gate_srtq256n512t1024_kernel(tc, qT, k_words, k_scales,
         q_rows = qT[0].rearrange("(p j) q -> p j q", j=PACK)
         q_raw = [tile(f"q_raw{i}", [P, PACK, P], F32) for i in range(QT)]
         nc.sync.dma_start(q_raw[0][:], q_rows[:, :, 0:P])
-        nc.sync.dma_start(kw_pool[:, PREFIX:T], kw_rows[:, PREFIX:T])
         nc.sync.dma_start(q_raw[1][:], q_rows[:, :, P:NQ])
+        nc.sync.dma_start(kw_pool[:, PREFIX:T], kw_rows[:, PREFIX:T])
         nc.sync.dma_start(vs_pool[0:1, :], vs[0:1, :])
         v_pool = tile("v_pool", [P, T], F32)
         nc.sync.dma_start(v_pool[:], vT)
@@ -80,13 +80,21 @@ def tile_attend_soft_cap_gate_srtq256n512t1024_kernel(tc, qT, k_words, k_scales,
 
         th = []
         for i in range(QT):
-            score = ps.tile([P, N], F32, name=f"score{i}")
+            th.append(tile(f"th{i}", [P, PACK, P], F32))
+            if i == 0:
+                banks = [ps.tile([P, H], F32, name=f"score0{h}", tag=f"score0{h}")[:] for h in range(2)]
+            else:
+                score = ps.tile([P, N], F32, name="score1")
+                banks = [score[:, 0:H], score[:, H:N]]
             for h in range(2):
                 cols = slice(h * H, (h + 1) * H)
-                nc.tensor.matmul_mx(score[:, cols], lhsT=q_codes[i][:].bitcast(FP8X4), lhsT_scale=q_scales[i][:],
+                nc.tensor.matmul_mx(banks[h], lhsT=q_codes[i][:].bitcast(FP8X4), lhsT_scale=q_scales[i][:],
                                     rhs=kw_g[h][:].bitcast(FP8X4), rhs_scale=ks_g[:, cols], start=True, stop=True)
-            th.append(tile(f"th{i}", [P, PACK, P], F32))
-            nc.scalar.activation(th[i][:], score[:].rearrange("p (s t) -> p t s", t=PACK), ACT.Tanh, scale=1.0 / CAP)
+                if i == 0:
+                    nc.scalar.activation(th[i][:, :, h * 64 : (h + 1) * 64], banks[h].rearrange("p (s t) -> p t s", t=PACK),
+                                         ACT.Tanh, scale=1.0 / CAP)
+            if i == 1:
+                nc.scalar.activation(th[i][:], score[:].rearrange("p (s t) -> p t s", t=PACK), ACT.Tanh, scale=1.0 / CAP)
 
         vs_t = ps.tile([P, PACK, P], F32, name="vs_t")
         for t in range(PACK):
@@ -143,12 +151,12 @@ def tile_attend_soft_cap_gate_srtq256n512t1024_kernel(tc, qT, k_words, k_scales,
         nc.scalar.activation(gate_th[:], og_sb[:], ACT.Tanh, scale=0.5)
         gate = tile("gate", [P, QT, DV], F32)
         nc.scalar.activation(gate[:], gate_th[:], ACT.Copy, scale=0.5, bias=0.5)
-        inv = tile("inv", [P, QT], F32)
+        inv = tile("inv", [P, QT], F32, tag="w_bf1")
         nc.vector.reciprocal(inv[:], total[:])
 
         for i in range(QT):
             cols = slice(i * P, (i + 1) * P)
-            y = ps.tile([P, DV], F32, name=f"y{i}")
+            y = ps.tile([P, DV], F32, name=f"y{i}", tag=f"score0{i}")
             nc.tensor.matmul_mx(y[:], lhsT=w_codes[i][:].bitcast(FP8X4), lhsT_scale=w_scales[i][:],
                                 rhs=v_codes[:].bitcast(FP8X4), rhs_scale=v_scales[:], start=True, stop=True)
             res = tile(f"res{i}", [P, DV], F32)

@@ -42,7 +42,7 @@ def tile_attend_soft_cap_gate_srtq256n512t1024_kernel(tc, qT, k_words, k_scales,
         kw_rows = k_words[0].rearrange("p n t -> p (n t)").bitcast(I32)
         nc.sync.dma_start(kw_pool[:, 0:PREFIX], kw_rows[:, 0:PREFIX])
         ks_pool = tile("ks_pool", [P, T], U8)
-        nc.vector.memset(ks_pool[:].bitcast(I32), 0)
+        nc.gpsimd.memset(ks_pool[:].bitcast(I32), 0)
         for r in range(4):
             (nc.scalar if r % 2 else nc.sync).dma_start(ks_pool[r:P:32, :].bitcast(I32), k_scales[0, r:16:4, :].bitcast(I32))
         vs_pool = tile("vs_pool", [P, T], F32)
@@ -81,20 +81,13 @@ def tile_attend_soft_cap_gate_srtq256n512t1024_kernel(tc, qT, k_words, k_scales,
         th = []
         for i in range(QT):
             th.append(tile(f"th{i}", [P, PACK, P], F32))
-            if i == 0:
-                banks = [ps.tile([P, H], F32, name=f"score0{h}", tag=f"score0{h}")[:] for h in range(2)]
-            else:
-                score = ps.tile([P, N], F32, name="score1")
-                banks = [score[:, 0:H], score[:, H:N]]
             for h in range(2):
                 cols = slice(h * H, (h + 1) * H)
-                nc.tensor.matmul_mx(banks[h], lhsT=q_codes[i][:].bitcast(FP8X4), lhsT_scale=q_scales[i][:],
+                score = ps.tile([P, H], F32, name=f"score{i}{h}", tag=f"score{i}{h}")
+                nc.tensor.matmul_mx(score[:], lhsT=q_codes[i][:].bitcast(FP8X4), lhsT_scale=q_scales[i][:],
                                     rhs=kw_g[h][:].bitcast(FP8X4), rhs_scale=ks_g[:, cols], start=True, stop=True)
-                if i == 0:
-                    nc.scalar.activation(th[i][:, :, h * 64 : (h + 1) * 64], banks[h].rearrange("p (s t) -> p t s", t=PACK),
-                                         ACT.Tanh, scale=1.0 / CAP)
-            if i == 1:
-                nc.scalar.activation(th[i][:], score[:].rearrange("p (s t) -> p t s", t=PACK), ACT.Tanh, scale=1.0 / CAP)
+                nc.scalar.activation(th[i][:, :, h * 64 : (h + 1) * 64], score[:].rearrange("p (s t) -> p t s", t=PACK),
+                                     ACT.Tanh, scale=1.0 / CAP)
 
         vs_t = ps.tile([P, PACK, P], F32, name="vs_t")
         for t in range(PACK):

@@ -109,12 +109,12 @@ def tile_attend_soft_cap_gate_srtq256n512t1024_kernel(tc, qT, k_words, k_scales,
                     cols = slice(h * H, (h + 1) * H)
                     nc.scalar.activation(p[i][:, cols], neg_c[:, cols], ACT.Exp, bias=neg_m[:], scale=-1.0,
                                          accum_out=parts[:, h : h + 1])
+                vs_col = tile("vs_col", [P, PACK], F32, tag="neg_c1")
+                nc.scalar.copy(vs_col[:], vs_t[:, :, 0])
                 nc.scalar.activation(total[:, 1:2], parts[:, 0:1], ACT.Identity, bias=parts[:, 1:2])
 
         v_g = tile("v_g", [P, N], BF16, tag="neg_c0")
         nc.vector.tensor_copy(v_g[:], v_pool[:].indirect(offsets[:]))
-        vs_col = tile("vs_col", [P, PACK], F32, tag="th1")
-        nc.scalar.copy(vs_col[:], vs_t[:, :, 0])
 
         w_bf = []
         for i in range(QT):
@@ -140,7 +140,7 @@ def tile_attend_soft_cap_gate_srtq256n512t1024_kernel(tc, qT, k_words, k_scales,
         quantise(v_codes[:], v_scales[:], v_bf[:])
         quantise(w_codes[1][:], w_scales[1][:], w_bf[1][:])
 
-        gate_th = tile("gate_th", [P, QT, DV], F32, tag="neg_c1")
+        gate_th = tile("gate_th", [P, QT, DV], F32, tag="parts")
         nc.scalar.activation(gate_th[:], og_sb[:], ACT.Tanh, scale=0.5)
         gate = tile("gate", [P, QT, DV], F32)
         nc.scalar.activation(gate[:], gate_th[:], ACT.Copy, scale=0.5, bias=0.5)

@@ -64,7 +64,8 @@ def tile_attend_soft_cap_gate_srtq256n512t1024_kernel(tc, qT, k_words, k_scales,
         q_bf = []
         for i in range(QT):
             q_bf.append(tile(f"q_bf{i}", [P, P, PACK], BF16))
-            nc.scalar.activation(q_bf[i][:], q_raw[i][:].rearrange("p j q -> p q j"), ACT.Copy)
+            nc.scalar.activation(q_bf[i][:].rearrange("p (c n) j -> p c j n", n=4),
+                                 q_raw[i][:].rearrange("p j (c n) -> p c j n", n=4), ACT.Copy)
         q_codes = [tile(f"q_codes{i}", [P, P], U32) for i in range(QT)]
         q_scales = [tile(f"q_scales{i}", [P, P], U8) for i in range(QT)]
 
@@ -89,32 +90,30 @@ def tile_attend_soft_cap_gate_srtq256n512t1024_kernel(tc, qT, k_words, k_scales,
                 nc.scalar.activation(th[i][:, :, h * 64 : (h + 1) * 64], score[:].rearrange("p (s t) -> p t s", t=PACK),
                                      ACT.Tanh, scale=1.0 / CAP)
 
-        vs_t = ps.tile([P, PACK, P], F32, name="vs_t")
+        vs_t = ps.tile([P, PACK, P], F32, name="vs_t", tag="vs_t")
         for t in range(PACK):
             nc.tensor.transpose(vs_t[:, t, :], vs_g[:, t:N:PACK], ident[:])
 
         total = tile("total", [P, QT], F32)
-        parts = tile("parts", [P, 2], F32)
-        p = []
+        parts = tile("parts", [P, QT, 2], F32)
+        p, neg_c = [], []
         for i in range(QT):
-            neg_c = tile(f"neg_c{i}", [P, N], F32)
+            neg_c.append(tile(f"neg_c{i}", [P, N], F32))
             neg_m = tile(f"neg_m{i}", [P, 1], F32)
-            nc.vector.tensor_scalar(neg_c[:], th[i][:].rearrange("p t s -> p (t s)"), -CAP, None, ALU.mult, ALU.min,
+            nc.vector.tensor_scalar(neg_c[i][:], th[i][:].rearrange("p t s -> p (t s)"), -CAP, None, ALU.mult, ALU.min,
                                     accum_out=neg_m[:])
             p.append(tile(f"p{i}", [P, N], F32))
-            if i == 0:
-                nc.scalar.activation(p[i][:], neg_c[:], ACT.Exp, bias=neg_m[:], scale=-1.0, accum_out=total[:, 0:1])
-            else:
-                for h in range(2):
-                    cols = slice(h * H, (h + 1) * H)
-                    nc.scalar.activation(p[i][:, cols], neg_c[:, cols], ACT.Exp, bias=neg_m[:], scale=-1.0,
-                                         accum_out=parts[:, h : h + 1])
-                vs_col = tile("vs_col", [P, PACK], F32, tag="neg_c1")
-                nc.scalar.copy(vs_col[:], vs_t[:, :, 0])
-                nc.scalar.activation(total[:, 1:2], parts[:, 0:1], ACT.Identity, bias=parts[:, 1:2])
+            for h in range(2):
+                cols = slice(h * H, (h + 1) * H)
+                nc.scalar.activation(p[i][:, cols], neg_c[i][:, cols], ACT.Exp, bias=neg_m[:], scale=-1.0,
+                                     accum_out=parts[:, i, h : h + 1])
+        vs_col = tile("vs_col", [P, PACK], F32, tag="neg_c1")
+        nc.scalar.copy(vs_col[:], vs_t[:, :, 0])
+        for i in range(QT):
+            nc.scalar.activation(total[:, i : i + 1], parts[:, i, 0:1], ACT.Identity, bias=parts[:, i, 1:2])
 
-        v_g = tile("v_g", [P, N], BF16, tag="neg_c0")
-        nc.vector.tensor_copy(v_g[:], v_pool[:].indirect(offsets[:]))
+        v_words = neg_c[0][:, 0:H]
+        nc.vector.tensor_copy(v_words.bitcast(BF16), v_pool[:].indirect(offsets[:]))
 
         w_bf = []
         for i in range(QT):
@@ -125,8 +124,7 @@ def tile_attend_soft_cap_gate_srtq256n512t1024_kernel(tc, qT, k_words, k_scales,
             nc.vector.tensor_tensor(w_bf[i][:], p_t[:].rearrange("p t q -> p q t"),
                                     vs_col[:].unsqueeze(1).to_broadcast([P, P, PACK]), ALU.mult)
 
-        v_t = ps.tile([P, 2, DV], F32, name="v_t")
-        v_words = v_g[:].bitcast(F32)
+        v_t = ps.tile([P, 2, DV], F32, name="v_t", tag="vs_t")
         for u in range(2):
             nc.tensor.transpose(v_t[:, u, :], v_words[:, u:H:2], ident[:])
         v_bf = tile("v_bf", [P, DV, PACK], BF16)

@@ -40,16 +40,16 @@ def tile_attend_soft_cap_gate_srtq256n512t1024_kernel(tc, qT, k_words, k_scales,
         nc.sync.dma_start(offsets[:], offs)
         kw_pool = tile("kw_pool", [P, T], I32)
         kw_rows = k_words[0].rearrange("p n t -> p (n t)").bitcast(I32)
-        nc.sync.dma_start(kw_pool[:, 0:PREFIX], kw_rows[:, 0:PREFIX])
+        q_rows = qT[0].rearrange("(p j) q -> p j q", j=PACK)
+        q_raw = [tile(f"q_raw{i}", [P, PACK, P], F32) for i in range(QT)]
+        nc.sync.dma_start(q_raw[0][:], q_rows[:, :, 0:P])
         ks_pool = tile("ks_pool", [P, T], U8)
         nc.gpsimd.memset(ks_pool[:].bitcast(I32), 0)
         for r in range(4):
             (nc.scalar if r % 2 else nc.sync).dma_start(ks_pool[r:P:32, :].bitcast(I32), k_scales[0, r:16:4, :].bitcast(I32))
         vs_pool = tile("vs_pool", [P, T], F32)
         nc.vector.memset(vs_pool[:].bitcast(I32), 0)
-        q_rows = qT[0].rearrange("(p j) q -> p j q", j=PACK)
-        q_raw = [tile(f"q_raw{i}", [P, PACK, P], F32) for i in range(QT)]
-        nc.sync.dma_start(q_raw[0][:], q_rows[:, :, 0:P])
+        nc.sync.dma_start(kw_pool[:, 0:PREFIX], kw_rows[:, 0:PREFIX])
         nc.sync.dma_start(q_raw[1][:], q_rows[:, :, P:NQ])
         nc.sync.dma_start(kw_pool[:, PREFIX:T], kw_rows[:, PREFIX:T])
         nc.sync.dma_start(vs_pool[0:1, :], vs[0:1, :])
@@ -70,10 +70,10 @@ def tile_attend_soft_cap_gate_srtq256n512t1024_kernel(tc, qT, k_words, k_scales,
         q_scales = [tile(f"q_scales{i}", [P, P], U8) for i in range(QT)]
 
         kw_g = [tile("kw_g0", [P, H], U32), tile("kw_g1", [P, H], U32, tag="q_raw0")]
-        nc.vector.tensor_copy(kw_g[0][:], kw_pool[:, 0:PREFIX].bitcast(U32).indirect(offsets[:, 0 : H // 16]))
         ks_g = tile("ks_g", [P, N], U8)
         nc.vector.tensor_copy(ks_g[:], ks_pool[:].indirect(offsets[:]))
         quantise(q_codes[0][:], q_scales[0][:], q_bf[0][:])
+        nc.vector.tensor_copy(kw_g[0][:], kw_pool[:, 0:PREFIX].bitcast(U32).indirect(offsets[:, 0 : H // 16]))
         nc.vector.tensor_copy(kw_g[1][:], kw_pool[:].bitcast(U32).indirect(offsets[:, H // 16 : N // 16]))
         quantise(q_codes[1][:], q_scales[1][:], q_bf[1][:])
         vs_g = tile("vs_g", [P, N], F32, tag="q_raw1")
@@ -96,18 +96,19 @@ def tile_attend_soft_cap_gate_srtq256n512t1024_kernel(tc, qT, k_words, k_scales,
 
         total = tile("total", [P, QT], F32)
         parts = tile("parts", [P, QT, 2], F32)
+        neg_both = tile("neg_both", [P, QT * N], F32, tag="vs_pool")
         p, neg_c = [], []
         for i in range(QT):
-            neg_c.append(tile(f"neg_c{i}", [P, N], F32))
+            neg_c.append(neg_both[:, i * N : (i + 1) * N])
             neg_m = tile(f"neg_m{i}", [P, 1], F32)
-            nc.vector.tensor_scalar(neg_c[i][:], th[i][:].rearrange("p t s -> p (t s)"), -CAP, None, ALU.mult, ALU.min,
+            nc.vector.tensor_scalar(neg_c[i], th[i][:].rearrange("p t s -> p (t s)"), -CAP, None, ALU.mult, ALU.min,
                                     accum_out=neg_m[:])
             p.append(tile(f"p{i}", [P, N], F32))
             for h in range(2):
                 cols = slice(h * H, (h + 1) * H)
                 nc.scalar.activation(p[i][:, cols], neg_c[i][:, cols], ACT.Exp, bias=neg_m[:], scale=-1.0,
                                      accum_out=parts[:, i, h : h + 1])
-        vs_col = tile("vs_col", [P, PACK], F32, tag="neg_c1")
+        vs_col = tile("vs_col", [P, PACK], F32, tag="neg_m1")
         nc.scalar.copy(vs_col[:], vs_t[:, :, 0])
         for i in range(QT):
             nc.scalar.activation(total[:, i : i + 1], parts[:, i, 0:1], ACT.Identity, bias=parts[:, i, 1:2])
@@ -115,13 +116,13 @@ def tile_attend_soft_cap_gate_srtq256n512t1024_kernel(tc, qT, k_words, k_scales,
         v_words = neg_c[0][:, 0:H]
         nc.vector.tensor_copy(v_words.bitcast(BF16), v_pool[:].indirect(offsets[:]))
 
-        w_bf = []
+        w_both = tile("w_both", [P, QT * N], BF16, tag="v_pool")
+        w_bf = [w_both[:, i * N : (i + 1) * N].rearrange("p (q t) -> p q t", t=PACK) for i in range(QT)]
         for i in range(QT):
             p_t = ps.tile([P, PACK, P], F32, name=f"p_t{i}")
             for t in range(PACK):
                 nc.tensor.transpose(p_t[:, t, :], p[i][:, t * P : (t + 1) * P], ident[:])
-            w_bf.append(tile(f"w_bf{i}", [P, P, PACK], BF16))
-            nc.vector.tensor_tensor(w_bf[i][:], p_t[:].rearrange("p t q -> p q t"),
+            nc.vector.tensor_tensor(w_bf[i], p_t[:].rearrange("p t q -> p q t"),
                                     vs_col[:].unsqueeze(1).to_broadcast([P, P, PACK]), ALU.mult)
 
         v_t = ps.tile([P, 2, DV], F32, name="v_t", tag="vs_t")
@@ -134,15 +135,15 @@ def tile_attend_soft_cap_gate_srtq256n512t1024_kernel(tc, qT, k_words, k_scales,
         v_scales = tile("v_scales", [P, DV], U8)
         w_codes = [tile("w_codes0", [P, P], U32, tag="p1"), tile("w_codes1", [P, P], U32)]
         w_scales = [tile(f"w_scales{i}", [P, P], U8) for i in range(QT)]
-        quantise(w_codes[0][:], w_scales[0][:], w_bf[0][:])
+        quantise(w_codes[0][:], w_scales[0][:], w_bf[0])
         quantise(v_codes[:], v_scales[:], v_bf[:])
-        quantise(w_codes[1][:], w_scales[1][:], w_bf[1][:])
+        quantise(w_codes[1][:], w_scales[1][:], w_bf[1])
 
         gate_th = tile("gate_th", [P, QT, DV], F32, tag="parts")
         nc.scalar.activation(gate_th[:], og_sb[:], ACT.Tanh, scale=0.5)
         gate = tile("gate", [P, QT, DV], F32)
         nc.scalar.activation(gate[:], gate_th[:], ACT.Copy, scale=0.5, bias=0.5)
-        inv = tile("inv", [P, QT], F32, tag="w_bf1")
+        inv = tile("inv", [P, QT], F32, tag="v_pool")
         nc.vector.reciprocal(inv[:], total[:])
 
         for i in range(QT):

@@ -49,8 +49,8 @@ def tile_attend_soft_cap_gate_srtq256n512t1024_kernel(tc, qT, k_words, k_scales,
             (nc.scalar if r % 2 else nc.sync).dma_start(ks_pool[r:P:32, :].bitcast(I32), k_scales[0, r:16:4, :].bitcast(I32))
         vs_pool = tile("vs_pool", [P, T], F32)
         nc.vector.memset(vs_pool[:].bitcast(I32), 0)
-        nc.sync.dma_start(kw_pool[:, 0:PREFIX], kw_rows[:, 0:PREFIX])
         nc.sync.dma_start(q_raw[1][:], q_rows[:, :, P:NQ])
+        nc.sync.dma_start(kw_pool[:, 0:PREFIX], kw_rows[:, 0:PREFIX])
         nc.sync.dma_start(kw_pool[:, PREFIX:T], kw_rows[:, PREFIX:T])
         nc.sync.dma_start(vs_pool[0:1, :], vs[0:1, :])
         v_pool = tile("v_pool", [P, T], F32)
@@ -73,15 +73,17 @@ def tile_attend_soft_cap_gate_srtq256n512t1024_kernel(tc, qT, k_words, k_scales,
         ks_g = tile("ks_g", [P, N], U8)
         nc.vector.tensor_copy(ks_g[:], ks_pool[:].indirect(offsets[:]))
         quantise(q_codes[0][:], q_scales[0][:], q_bf[0][:])
+        quantise(q_codes[1][:], q_scales[1][:], q_bf[1][:])
         nc.vector.tensor_copy(kw_g[0][:], kw_pool[:, 0:PREFIX].bitcast(U32).indirect(offsets[:, 0 : H // 16]))
         nc.vector.tensor_copy(kw_g[1][:], kw_pool[:].bitcast(U32).indirect(offsets[:, H // 16 : N // 16]))
-        quantise(q_codes[1][:], q_scales[1][:], q_bf[1][:])
         vs_g = tile("vs_g", [P, N], F32, tag="q_raw1")
-        nc.vector.tensor_copy(vs_g[:], vs_pool[:].indirect(offsets[:]))
+        nc.scalar.activation(vs_g[:], vs_pool[:].indirect(offsets[:]), ACT.Copy)
+        v_words = tile("v_words", [P, H], F32)
+        nc.vector.tensor_copy(v_words[:].bitcast(BF16), v_pool[:].indirect(offsets[:]))
 
-        th = []
+        th_both = tile("th_both", [P, QT * N], F32, tag="vs_pool")
+        th = [th_both[:, i * N : (i + 1) * N].rearrange("p (t s) -> p t s", t=PACK) for i in range(QT)]
         for i in range(QT):
-            th.append(tile(f"th{i}", [P, PACK, P], F32))
             for h in range(2):
                 cols = slice(h * H, (h + 1) * H)
                 score = ps.tile([P, H], F32, name=f"score{i}{h}", tag=f"score{i}{h}")
@@ -93,31 +95,31 @@ def tile_attend_soft_cap_gate_srtq256n512t1024_kernel(tc, qT, k_words, k_scales,
         vs_t = ps.tile([P, PACK, P], F32, name="vs_t", tag="vs_t")
         for t in range(PACK):
             nc.tensor.transpose(vs_t[:, t, :], vs_g[:, t:N:PACK], ident[:])
+        vs_col = tile("vs_col", [P, PACK], F32)
+        nc.scalar.copy(vs_col[:], vs_t[:, :, 0])
+        v_t = ps.tile([P, 2, DV], F32, name="v_t")
+        for u in range(2):
+            nc.tensor.transpose(v_t[:, u, :], v_words[:, u:H:2], ident[:])
 
         total = tile("total", [P, QT], F32)
         parts = tile("parts", [P, QT, 2], F32)
-        neg_both = tile("neg_both", [P, QT * N], F32, tag="vs_pool")
         p, neg_c = [], []
         for i in range(QT):
-            neg_c.append(neg_both[:, i * N : (i + 1) * N])
+            neg_c.append(tile(f"neg_c{i}", [P, N], F32)[:])
             neg_m = tile(f"neg_m{i}", [P, 1], F32)
-            nc.vector.tensor_scalar(neg_c[i], th[i][:].rearrange("p t s -> p (t s)"), -CAP, None, ALU.mult, ALU.min,
+            nc.vector.tensor_scalar(neg_c[i], th_both[:, i * N : (i + 1) * N], -CAP, None, ALU.mult, ALU.min,
                                     accum_out=neg_m[:])
             p.append(tile(f"p{i}", [P, N], F32))
             for h in range(2):
                 cols = slice(h * H, (h + 1) * H)
                 nc.scalar.activation(p[i][:, cols], neg_c[i][:, cols], ACT.Exp, bias=neg_m[:], scale=-1.0,
                                      accum_out=parts[:, i, h : h + 1])
-        vs_col = tile("vs_col", [P, PACK], F32, tag="neg_m1")
-        nc.scalar.copy(vs_col[:], vs_t[:, :, 0])
+        v_bf = tile("v_bf", [P, DV, PACK], BF16, tag="vs_pool")
+        nc.vector.tensor_copy(v_bf[:].bitcast(F32), v_t[:].rearrange("p u e -> p e u"))
         for i in range(QT):
             nc.scalar.activation(total[:, i : i + 1], parts[:, i, 0:1], ACT.Identity, bias=parts[:, i, 1:2])
 
-        v_words = neg_c[0][:, 0:H]
-        nc.vector.tensor_copy(v_words.bitcast(BF16), v_pool[:].indirect(offsets[:]))
-
-        w_both = tile("w_both", [P, QT * N], BF16, tag="v_pool")
-        w_bf = [w_both[:, i * N : (i + 1) * N].rearrange("p (q t) -> p q t", t=PACK) for i in range(QT)]
+        w_bf = [tile(f"w_bf{i}", [P, P, PACK], BF16)[:] for i in range(QT)]
         for i in range(QT):
             p_t = ps.tile([P, PACK, P], F32, name=f"p_t{i}")
             for t in range(PACK):
@@ -125,15 +127,9 @@ def tile_attend_soft_cap_gate_srtq256n512t1024_kernel(tc, qT, k_words, k_scales,
             nc.vector.tensor_tensor(w_bf[i], p_t[:].rearrange("p t q -> p q t"),
                                     vs_col[:].unsqueeze(1).to_broadcast([P, P, PACK]), ALU.mult)
 
-        v_t = ps.tile([P, 2, DV], F32, name="v_t", tag="vs_t")
-        for u in range(2):
-            nc.tensor.transpose(v_t[:, u, :], v_words[:, u:H:2], ident[:])
-        v_bf = tile("v_bf", [P, DV, PACK], BF16)
-        nc.scalar.copy(v_bf[:].bitcast(F32), v_t[:].rearrange("p u e -> p e u"))
-
         v_codes = tile("v_codes", [P, DV], U32)
         v_scales = tile("v_scales", [P, DV], U8)
-        w_codes = [tile("w_codes0", [P, P], U32, tag="p1"), tile("w_codes1", [P, P], U32)]
+        w_codes = [tile("w_codes0", [P, P], U32), tile("w_codes1", [P, P], U32)]
         w_scales = [tile(f"w_scales{i}", [P, P], U8) for i in range(QT)]
         quantise(w_codes[0][:], w_scales[0][:], w_bf[0])
         quantise(v_codes[:], v_scales[:], v_bf[:])
@@ -143,7 +139,7 @@ def tile_attend_soft_cap_gate_srtq256n512t1024_kernel(tc, qT, k_words, k_scales,
         nc.scalar.activation(gate_th[:], og_sb[:], ACT.Tanh, scale=0.5)
         gate = tile("gate", [P, QT, DV], F32)
         nc.scalar.activation(gate[:], gate_th[:], ACT.Copy, scale=0.5, bias=0.5)
-        inv = tile("inv", [P, QT], F32, tag="v_pool")
+        inv = tile("inv", [P, QT], F32, tag="w_bf1")
         nc.vector.reciprocal(inv[:], total[:])
 
         for i in range(QT):

@@ -21,6 +21,10 @@ P = 128
 PACK = 4
 QT = NQ // P
 H = N // 2
+PER_COLUMN = 16
+QUADRANT = 32
+LINE = 4
+SPLIT = 3 * N // 4
 PREFIX = T - (N - H)
 
 
@@ -36,17 +40,21 @@ def tile_attend_soft_cap_gate_srtq256n512t1024_kernel(tc, qT, k_words, k_scales,
         def quantise(codes, scales, grouped):
             nc.vector.quantize_mx(codes.bitcast(FP8X4), scales, grouped.rearrange("p c j -> p (c j)"))
 
-        offsets = sb.tile([P, N // 16], U16, name="offsets")
+        def entries(first, last):
+            return offsets[:, first // PER_COLUMN : last // PER_COLUMN]
+
+        offsets = sb.tile([P, N // PER_COLUMN], U16, name="offsets")
         nc.sync.dma_start(offsets[:], offs)
         kw_pool = tile("kw_pool", [P, T], I32)
         kw_rows = k_words[0].rearrange("p n t -> p (n t)").bitcast(I32)
         q_rows = qT[0].rearrange("(p j) q -> p j q", j=PACK)
         q_raw = [tile(f"q_raw{i}", [P, PACK, P], F32) for i in range(QT)]
-        nc.sync.dma_start(q_raw[0][:], q_rows[:, :, 0:P])
+        nc.scalar.dma_start(q_raw[0][:], q_rows[:, :, 0:P])
         ks_pool = tile("ks_pool", [P, T], U8)
         nc.gpsimd.memset(ks_pool[:].bitcast(I32), 0)
-        for r in range(4):
-            (nc.scalar if r % 2 else nc.sync).dma_start(ks_pool[r:P:32, :].bitcast(I32), k_scales[0, r:16:4, :].bitcast(I32))
+        for r in range(PACK):
+            queue = nc.scalar if r % 2 else nc.sync
+            queue.dma_start(ks_pool[r:P:QUADRANT, :].bitcast(I32), k_scales[0, r : D // 32 : PACK, :].bitcast(I32))
         vs_pool = tile("vs_pool", [P, T], F32)
         nc.vector.memset(vs_pool[:].bitcast(I32), 0)
         nc.sync.dma_start(q_raw[1][:], q_rows[:, :, P:NQ])
@@ -64,8 +72,8 @@ def tile_attend_soft_cap_gate_srtq256n512t1024_kernel(tc, qT, k_words, k_scales,
         q_bf = []
         for i in range(QT):
             q_bf.append(tile(f"q_bf{i}", [P, P, PACK], BF16))
-            nc.scalar.activation(q_bf[i][:].rearrange("p (c n) j -> p c j n", n=4),
-                                 q_raw[i][:].rearrange("p j (c n) -> p c j n", n=4), ACT.Copy)
+            nc.scalar.activation(q_bf[i][:].rearrange("p (c n) j -> p c j n", n=LINE),
+                                 q_raw[i][:].rearrange("p j (c n) -> p c j n", n=LINE), ACT.Copy)
         q_codes = [tile(f"q_codes{i}", [P, P], U32) for i in range(QT)]
         q_scales = [tile(f"q_scales{i}", [P, P], U8) for i in range(QT)]
 
@@ -74,10 +82,11 @@ def tile_attend_soft_cap_gate_srtq256n512t1024_kernel(tc, qT, k_words, k_scales,
         nc.vector.tensor_copy(ks_g[:], ks_pool[:].indirect(offsets[:]))
         quantise(q_codes[0][:], q_scales[0][:], q_bf[0][:])
         quantise(q_codes[1][:], q_scales[1][:], q_bf[1][:])
-        nc.vector.tensor_copy(kw_g[0][:], kw_pool[:, 0:PREFIX].bitcast(U32).indirect(offsets[:, 0 : H // 16]))
-        nc.vector.tensor_copy(kw_g[1][:], kw_pool[:].bitcast(U32).indirect(offsets[:, H // 16 : N // 16]))
+        nc.vector.tensor_copy(kw_g[0][:], kw_pool[:, 0:PREFIX].bitcast(U32).indirect(entries(0, H)))
+        nc.vector.tensor_copy(kw_g[1][:], kw_pool[:].bitcast(U32).indirect(entries(H, N)))
         vs_g = tile("vs_g", [P, N], F32, tag="q_raw1")
-        nc.scalar.activation(vs_g[:], vs_pool[:].indirect(offsets[:]), ACT.Copy)
+        nc.scalar.activation(vs_g[:, 0:SPLIT], vs_pool[:].indirect(entries(0, SPLIT)), ACT.Copy)
+        nc.vector.tensor_copy(vs_g[:, SPLIT:N], vs_pool[:].indirect(entries(SPLIT, N)))
         v_words = tile("v_words", [P, H], F32)
         nc.vector.tensor_copy(v_words[:].bitcast(BF16), v_pool[:].indirect(offsets[:]))
 
@@ -85,12 +94,12 @@ def tile_attend_soft_cap_gate_srtq256n512t1024_kernel(tc, qT, k_words, k_scales,
         th = [th_both[:, i * N : (i + 1) * N].rearrange("p (t s) -> p t s", t=PACK) for i in range(QT)]
         for i in range(QT):
             for h in range(2):
-                cols = slice(h * H, (h + 1) * H)
                 score = ps.tile([P, H], F32, name=f"score{i}{h}", tag=f"score{i}{h}")
                 nc.tensor.matmul_mx(score[:], lhsT=q_codes[i][:].bitcast(FP8X4), lhsT_scale=q_scales[i][:],
-                                    rhs=kw_g[h][:].bitcast(FP8X4), rhs_scale=ks_g[:, cols], start=True, stop=True)
-                nc.scalar.activation(th[i][:, :, h * 64 : (h + 1) * 64], score[:].rearrange("p (s t) -> p t s", t=PACK),
-                                     ACT.Tanh, scale=1.0 / CAP)
+                                    rhs=kw_g[h][:].bitcast(FP8X4), rhs_scale=ks_g[:, h * H : (h + 1) * H],
+                                    start=True, stop=True)
+                nc.scalar.activation(th[i][:, :, h * H // PACK : (h + 1) * H // PACK],
+                                     score[:].rearrange("p (s t) -> p t s", t=PACK), ACT.Tanh, scale=1.0 / CAP)
 
         vs_t = ps.tile([P, PACK, P], F32, name="vs_t", tag="vs_t")
         for t in range(PACK):
@@ -103,37 +112,37 @@ def tile_attend_soft_cap_gate_srtq256n512t1024_kernel(tc, qT, k_words, k_scales,
 
         total = tile("total", [P, QT], F32)
         parts = tile("parts", [P, QT, 2], F32)
-        p, neg_c = [], []
+        p = []
         for i in range(QT):
-            neg_c.append(tile(f"neg_c{i}", [P, N], F32)[:])
+            neg_c = tile(f"neg_c{i}", [P, N], F32)
             neg_m = tile(f"neg_m{i}", [P, 1], F32)
-            nc.vector.tensor_scalar(neg_c[i], th_both[:, i * N : (i + 1) * N], -CAP, None, ALU.mult, ALU.min,
+            nc.vector.tensor_scalar(neg_c[:], th_both[:, i * N : (i + 1) * N], -CAP, None, ALU.mult, ALU.min,
                                     accum_out=neg_m[:])
             p.append(tile(f"p{i}", [P, N], F32))
             for h in range(2):
-                cols = slice(h * H, (h + 1) * H)
-                nc.scalar.activation(p[i][:, cols], neg_c[i][:, cols], ACT.Exp, bias=neg_m[:], scale=-1.0,
+                places = slice(h * H, (h + 1) * H)
+                nc.scalar.activation(p[i][:, places], neg_c[:, places], ACT.Exp, bias=neg_m[:], scale=-1.0,
                                      accum_out=parts[:, i, h : h + 1])
         v_bf = tile("v_bf", [P, DV, PACK], BF16, tag="vs_pool")
         nc.vector.tensor_copy(v_bf[:].bitcast(F32), v_t[:].rearrange("p u e -> p e u"))
         for i in range(QT):
             nc.scalar.activation(total[:, i : i + 1], parts[:, i, 0:1], ACT.Identity, bias=parts[:, i, 1:2])
 
-        w_bf = [tile(f"w_bf{i}", [P, P, PACK], BF16)[:] for i in range(QT)]
+        w_bf = [tile(f"w_bf{i}", [P, P, PACK], BF16) for i in range(QT)]
         for i in range(QT):
             p_t = ps.tile([P, PACK, P], F32, name=f"p_t{i}")
             for t in range(PACK):
                 nc.tensor.transpose(p_t[:, t, :], p[i][:, t * P : (t + 1) * P], ident[:])
-            nc.vector.tensor_tensor(w_bf[i], p_t[:].rearrange("p t q -> p q t"),
+            nc.vector.tensor_tensor(w_bf[i][:], p_t[:].rearrange("p t q -> p q t"),
                                     vs_col[:].unsqueeze(1).to_broadcast([P, P, PACK]), ALU.mult)
 
         v_codes = tile("v_codes", [P, DV], U32)
         v_scales = tile("v_scales", [P, DV], U8)
-        w_codes = [tile("w_codes0", [P, P], U32), tile("w_codes1", [P, P], U32)]
+        w_codes = [tile(f"w_codes{i}", [P, P], U32) for i in range(QT)]
         w_scales = [tile(f"w_scales{i}", [P, P], U8) for i in range(QT)]
-        quantise(w_codes[0][:], w_scales[0][:], w_bf[0])
+        quantise(w_codes[0][:], w_scales[0][:], w_bf[0][:])
         quantise(v_codes[:], v_scales[:], v_bf[:])
-        quantise(w_codes[1][:], w_scales[1][:], w_bf[1])
+        quantise(w_codes[1][:], w_scales[1][:], w_bf[1][:])
 
         gate_th = tile("gate_th", [P, QT, DV], F32, tag="parts")
         nc.scalar.activation(gate_th[:], og_sb[:], ACT.Tanh, scale=0.5)
@@ -143,10 +152,9 @@ def tile_attend_soft_cap_gate_srtq256n512t1024_kernel(tc, qT, k_words, k_scales,
         nc.vector.reciprocal(inv[:], total[:])
 
         for i in range(QT):
-            cols = slice(i * P, (i + 1) * P)
             y = ps.tile([P, DV], F32, name=f"y{i}", tag=f"score0{i}")
             nc.tensor.matmul_mx(y[:], lhsT=w_codes[i][:].bitcast(FP8X4), lhsT_scale=w_scales[i][:],
                                 rhs=v_codes[:].bitcast(FP8X4), rhs_scale=v_scales[:], start=True, stop=True)
             res = tile(f"res{i}", [P, DV], F32)
             nc.vector.scalar_tensor_tensor(res[:], y[:], inv[:, i : i + 1], gate[:, i, :], ALU.mult, ALU.mult)
-            (nc.sync if i == QT - 1 else nc.scalar).dma_start(out[0, cols, :], res[:])
+            (nc.sync if i == QT - 1 else nc.scalar).dma_start(out[0, i * P : (i + 1) * P, :], res[:])

@@ -51,10 +51,12 @@ def tile_attend_soft_cap_gate_srtq256n512t1024_kernel(tc, qT, k_words, k_scales,
         q_raw = [tile(f"q_raw{i}", [P, PACK, P], F32) for i in range(QT)]
         nc.scalar.dma_start(q_raw[0][:], q_rows[:, :, 0:P])
         ks_pool = tile("ks_pool", [P, T], U8)
-        nc.gpsimd.memset(ks_pool[:].bitcast(I32), 0)
+        nc.vector.memset(ks_pool[:].bitcast(I32), 0)
         for r in range(PACK):
             queue = nc.scalar if r % 2 else nc.sync
             queue.dma_start(ks_pool[r:P:QUADRANT, :].bitcast(I32), k_scales[0, r : D // 32 : PACK, :].bitcast(I32))
+        ident = tile("ident", [P, P], F32)
+        nc.vector.memset(ident[:], 0.0)
         vs_pool = tile("vs_pool", [P, T], F32)
         nc.vector.memset(vs_pool[:].bitcast(I32), 0)
         nc.sync.dma_start(q_raw[1][:], q_rows[:, :, P:NQ])
@@ -66,8 +68,7 @@ def tile_attend_soft_cap_gate_srtq256n512t1024_kernel(tc, qT, k_words, k_scales,
         og_sb = tile("og_sb", [P, QT, DV], F32)
         nc.sync.dma_start(og_sb[:], og[0].rearrange("(i p) e -> p i e", p=P))
 
-        ident = tile("ident", [P, P], F32)
-        make_identity(nc, ident[:])
+        make_identity(nc, ident[:], nomemset=True)
 
         q_bf = []
         for i in range(QT):

@@ -149,7 +149,7 @@ def tile_attend_soft_cap_gate_srtq256n512t1024_kernel(tc, qT, k_words, k_scales,
         nc.scalar.activation(gate_th[:], og_sb[:], ACT.Tanh, scale=0.5)
         gate = tile("gate", [P, QT, DV], F32)
         nc.scalar.activation(gate[:], gate_th[:], ACT.Copy, scale=0.5, bias=0.5)
-        inv = tile("inv", [P, QT], F32, tag="w_bf1")
+        inv = tile("inv", [P, QT], F32)
         nc.vector.reciprocal(inv[:], total[:])
 
         for i in range(QT):

@@ -102,11 +102,8 @@ def tile_attend_soft_cap_gate_srtq256n512t1024_kernel(tc, qT, k_words, k_scales,
                 nc.scalar.activation(th[i][:, :, h * H // PACK : (h + 1) * H // PACK],
                                      score[:].rearrange("p (s t) -> p t s", t=PACK), ACT.Tanh, scale=1.0 / CAP)
 
-        vs_t = ps.tile([P, PACK, P], F32, name="vs_t", tag="vs_t")
-        for t in range(PACK):
-            nc.tensor.transpose(vs_t[:, t, :], vs_g[:, t:N:PACK], ident[:])
         vs_col = tile("vs_col", [P, PACK], F32)
-        nc.scalar.copy(vs_col[:], vs_t[:, :, 0])
+        nc.sync.dma_start(vs_col[:], vs_g[0:1, :])
         v_t = ps.tile([P, 2, DV], F32, name="v_t")
         for u in range(2):
             nc.tensor.transpose(v_t[:, u, :], v_words[:, u:H:2], ident[:])

@@ -82,9 +82,9 @@ def tile_attend_soft_cap_gate_srtq256n512t1024_kernel(tc, qT, k_words, k_scales,
         ks_g = tile("ks_g", [P, N], U8)
         nc.vector.tensor_copy(ks_g[:], ks_pool[:].indirect(offsets[:]))
         quantise(q_codes[0][:], q_scales[0][:], q_bf[0][:])
-        quantise(q_codes[1][:], q_scales[1][:], q_bf[1][:])
         nc.vector.tensor_copy(kw_g[0][:], kw_pool[:, 0:PREFIX].bitcast(U32).indirect(entries(0, H)))
         nc.vector.tensor_copy(kw_g[1][:], kw_pool[:].bitcast(U32).indirect(entries(H, N)))
+        quantise(q_codes[1][:], q_scales[1][:], q_bf[1][:])
         vs_g = tile("vs_g", [P, N], F32, tag="q_raw1")
         nc.scalar.activation(vs_g[:, 0:SPLIT], vs_pool[:].indirect(entries(0, SPLIT)), ACT.Copy)
         nc.vector.tensor_copy(vs_g[:, SPLIT:N], vs_pool[:].indirect(entries(SPLIT, N)))

@@ -48,8 +48,8 @@ def tile_attend_soft_cap_gate_srtq256n512t1024_kernel(tc, qT, k_words, k_scales,
         kw_pool = tile("kw_pool", [P, T], I32)
         kw_rows = k_words[0].rearrange("p n t -> p (n t)").bitcast(I32)
         q_rows = qT[0].rearrange("(p j) q -> p j q", j=PACK)
-        q_raw = [tile(f"q_raw{i}", [P, PACK, P], F32) for i in range(QT)]
-        nc.scalar.dma_start(q_raw[0][:], q_rows[:, :, 0:P])
+        q_raw = tile("q_raw", [P, PACK, NQ], F32)
+        nc.scalar.dma_start(q_raw[:, 0:2, :], q_rows[:, 0:2, :])
         ks_pool = tile("ks_pool", [P, T], U8)
         nc.vector.memset(ks_pool[:].bitcast(I32), 0)
         for r in range(PACK):
@@ -59,7 +59,7 @@ def tile_attend_soft_cap_gate_srtq256n512t1024_kernel(tc, qT, k_words, k_scales,
         nc.vector.memset(ident[:], 0.0)
         vs_pool = tile("vs_pool", [P, T], F32)
         nc.vector.memset(vs_pool[:].bitcast(I32), 0)
-        nc.sync.dma_start(q_raw[1][:], q_rows[:, :, P:NQ])
+        nc.sync.dma_start(q_raw[:, 2:PACK, :], q_rows[:, 2:PACK, :])
         nc.sync.dma_start(kw_pool[:, 0:PREFIX], kw_rows[:, 0:PREFIX])
         nc.sync.dma_start(kw_pool[:, PREFIX:T], kw_rows[:, PREFIX:T])
         nc.sync.dma_start(vs_pool[0:1, :], vs[0:1, :])
@@ -70,22 +70,22 @@ def tile_attend_soft_cap_gate_srtq256n512t1024_kernel(tc, qT, k_words, k_scales,
 
         make_identity(nc, ident[:], nomemset=True)
 
-        q_bf = []
-        for i in range(QT):
-            q_bf.append(tile(f"q_bf{i}", [P, P, PACK], BF16))
-            nc.scalar.activation(q_bf[i][:].rearrange("p (c n) j -> p c j n", n=LINE),
-                                 q_raw[i][:].rearrange("p j (c n) -> p c j n", n=LINE), ACT.Copy)
+        q_bf = [tile(f"q_bf{i}", [P, P, PACK], BF16) for i in range(QT)]
+        for i, first, last in ((0, 0, 2), (0, 2, PACK), (1, 0, PACK)):
+            nc.scalar.activation(q_bf[i][:, :, first:last].rearrange("p (c n) j -> p c j n", n=LINE),
+                                 q_raw[:, first:last, i * P : (i + 1) * P].rearrange("p j (c n) -> p c j n", n=LINE),
+                                 ACT.Copy)
         q_codes = [tile(f"q_codes{i}", [P, P], U32) for i in range(QT)]
         q_scales = [tile(f"q_scales{i}", [P, P], U8) for i in range(QT)]
 
-        kw_g = [tile("kw_g0", [P, H], U32), tile("kw_g1", [P, H], U32, tag="q_raw0")]
+        kw_g = [tile("kw_g0", [P, H], U32), tile("kw_g1", [P, H], U32)]
         ks_g = tile("ks_g", [P, N], U8)
         nc.vector.tensor_copy(ks_g[:], ks_pool[:].indirect(offsets[:]))
         quantise(q_codes[0][:], q_scales[0][:], q_bf[0][:])
         nc.vector.tensor_copy(kw_g[0][:], kw_pool[:, 0:PREFIX].bitcast(U32).indirect(entries(0, H)))
         nc.vector.tensor_copy(kw_g[1][:], kw_pool[:].bitcast(U32).indirect(entries(H, N)))
         quantise(q_codes[1][:], q_scales[1][:], q_bf[1][:])
-        vs_g = tile("vs_g", [P, N], F32, tag="q_raw1")
+        vs_g = tile("vs_g", [P, N], F32, tag="q_raw")
         nc.scalar.activation(vs_g[:, 0:SPLIT], vs_pool[:].indirect(entries(0, SPLIT)), ACT.Copy)
         nc.vector.tensor_copy(vs_g[:, SPLIT:N], vs_pool[:].indirect(entries(SPLIT, N)))
         v_words = tile("v_words", [P, H], F32)

@@ -24,7 +24,6 @@ H = N // 2
 PER_COLUMN = 16
 QUADRANT = 32
 LINE = 4
-SPLIT = 3 * N // 4
 PREFIX = T - (N - H)
 
 
@@ -86,8 +85,7 @@ def tile_attend_soft_cap_gate_srtq256n512t1024_kernel(tc, qT, k_words, k_scales,
         nc.vector.tensor_copy(kw_g[1][:], kw_pool[:].bitcast(U32).indirect(entries(H, N)))
         quantise(q_codes[1][:], q_scales[1][:], q_bf[1][:])
         vs_g = tile("vs_g", [P, N], F32, tag="q_raw")
-        nc.scalar.activation(vs_g[:, 0:SPLIT], vs_pool[:].indirect(entries(0, SPLIT)), ACT.Copy)
-        nc.vector.tensor_copy(vs_g[:, SPLIT:N], vs_pool[:].indirect(entries(SPLIT, N)))
+        nc.scalar.activation(vs_g[:], vs_pool[:].indirect(offsets[:]), ACT.Copy)
         v_words = tile("v_words", [P, H], F32)
         nc.vector.tensor_copy(v_words[:].bitcast(BF16), v_pool[:].indirect(offsets[:]))
 

@@ -24,6 +24,7 @@ H = N // 2
 PER_COLUMN = 16
 QUADRANT = 32
 LINE = 4
+VS_ROW = 16
 PREFIX = T - (N - H)
 
 
@@ -61,7 +62,7 @@ def tile_attend_soft_cap_gate_srtq256n512t1024_kernel(tc, qT, k_words, k_scales,
         nc.sync.dma_start(q_raw[:, 2:PACK, :], q_rows[:, 2:PACK, :])
         nc.sync.dma_start(kw_pool[:, 0:PREFIX], kw_rows[:, 0:PREFIX])
         nc.sync.dma_start(kw_pool[:, PREFIX:T], kw_rows[:, PREFIX:T])
-        nc.sync.dma_start(vs_pool[0:1, :], vs[0:1, :])
+        nc.sync.dma_start(vs_pool[VS_ROW : VS_ROW + 1, :], vs[0:1, :])
         v_pool = tile("v_pool", [P, T], F32)
         nc.sync.dma_start(v_pool[:], vT)
         og_sb = tile("og_sb", [P, QT, DV], F32)
@@ -101,7 +102,7 @@ def tile_attend_soft_cap_gate_srtq256n512t1024_kernel(tc, qT, k_words, k_scales,
                                      score[:].rearrange("p (s t) -> p t s", t=PACK), ACT.Tanh, scale=1.0 / CAP)
 
         vs_col = tile("vs_col", [P, PACK], F32)
-        nc.sync.dma_start(vs_col[:], vs_g[0:1, :])
+        nc.sync.dma_start(vs_col[:], vs_g[VS_ROW : VS_ROW + 1, :])
         v_t = ps.tile([P, 2, DV], F32, name="v_t")
         for u in range(2):
             nc.tensor.transpose(v_t[:, u, :], v_words[:, u:H:2], ident[:])
@@ -129,8 +130,11 @@ def tile_attend_soft_cap_gate_srtq256n512t1024_kernel(tc, qT, k_words, k_scales,
             p_t = ps.tile([P, PACK, P], F32, name=f"p_t{i}")
             for t in range(PACK):
                 nc.tensor.transpose(p_t[:, t, :], p[i][:, t * P : (t + 1) * P], ident[:])
-            nc.vector.tensor_tensor(w_bf[i][:], p_t[:].rearrange("p t q -> p q t"),
-                                    vs_col[:].unsqueeze(1).to_broadcast([P, P, PACK]), ALU.mult)
+            width = P // 2 if i == QT - 1 else P
+            for first in range(0, P, width):
+                nc.vector.tensor_tensor(w_bf[i][:, first : first + width, :],
+                                        p_t[:, :, first : first + width].rearrange("p t q -> p q t"),
+                                        vs_col[:].unsqueeze(1).to_broadcast([P, width, PACK]), ALU.mult)
 
         v_codes = tile("v_codes", [P, DV], U32)
         v_scales = tile("v_scales", [P, DV], U8)
@@ -138,7 +142,9 @@ def tile_attend_soft_cap_gate_srtq256n512t1024_kernel(tc, qT, k_words, k_scales,
         w_scales = [tile(f"w_scales{i}", [P, P], U8) for i in range(QT)]
         quantise(w_codes[0][:], w_scales[0][:], w_bf[0][:])
         quantise(v_codes[:], v_scales[:], v_bf[:])
-        quantise(w_codes[1][:], w_scales[1][:], w_bf[1][:])
+        for first in range(0, P, P // 2):
+            columns = slice(first, first + P // 2)
+            quantise(w_codes[1][:, columns], w_scales[1][:, columns], w_bf[1][:, columns, :])
 
         gate_th = tile("gate_th", [P, QT, DV], F32, tag="parts")
         nc.scalar.activation(gate_th[:], og_sb[:], ACT.Tanh, scale=0.5)

@@ -25,6 +25,7 @@ PER_COLUMN = 16
 QUADRANT = 32
 LINE = 4
 VS_ROW = 16
+FIRST = 2 * NQ + P
 PREFIX = T - (N - H)
 
 
@@ -47,9 +48,10 @@ def tile_attend_soft_cap_gate_srtq256n512t1024_kernel(tc, qT, k_words, k_scales,
         nc.sync.dma_start(offsets[:], offs)
         kw_pool = tile("kw_pool", [P, T], I32)
         kw_rows = k_words[0].rearrange("p n t -> p (n t)").bitcast(I32)
-        q_rows = qT[0].rearrange("(p j) q -> p j q", j=PACK)
+        q_rows = qT[0].rearrange("(p j) q -> p (j q)", j=PACK)
         q_raw = tile("q_raw", [P, PACK, NQ], F32)
-        nc.scalar.dma_start(q_raw[:, 0:2, :], q_rows[:, 0:2, :])
+        q_flat = q_raw[:].rearrange("p j q -> p (j q)")
+        nc.scalar.dma_start(q_flat[:, 0:FIRST], q_rows[:, 0:FIRST])
         ks_pool = tile("ks_pool", [P, T], U8)
         nc.vector.memset(ks_pool[:].bitcast(I32), 0)
         for r in range(PACK):
@@ -59,7 +61,7 @@ def tile_attend_soft_cap_gate_srtq256n512t1024_kernel(tc, qT, k_words, k_scales,
         nc.vector.memset(ident[:], 0.0)
         vs_pool = tile("vs_pool", [P, T], F32)
         nc.vector.memset(vs_pool[:].bitcast(I32), 0)
-        nc.sync.dma_start(q_raw[:, 2:PACK, :], q_rows[:, 2:PACK, :])
+        nc.sync.dma_start(q_flat[:, FIRST : PACK * NQ], q_rows[:, FIRST : PACK * NQ])
         nc.sync.dma_start(kw_pool[:, 0:PREFIX], kw_rows[:, 0:PREFIX])
         nc.sync.dma_start(kw_pool[:, PREFIX:T], kw_rows[:, PREFIX:T])
         nc.sync.dma_start(vs_pool[VS_ROW : VS_ROW + 1, :], vs[0:1, :])
@@ -71,7 +73,7 @@ def tile_attend_soft_cap_gate_srtq256n512t1024_kernel(tc, qT, k_words, k_scales,
         make_identity(nc, ident[:], nomemset=True)
 
         q_bf = [tile(f"q_bf{i}", [P, P, PACK], BF16) for i in range(QT)]
-        for i, first, last in ((0, 0, 2), (0, 2, PACK), (1, 0, PACK)):
+        for i, first, last in ((0, 0, 3), (0, 3, PACK), (1, 0, PACK)):
             nc.scalar.activation(q_bf[i][:, :, first:last].rearrange("p (c n) j -> p c j n", n=LINE),
                                  q_raw[:, first:last, i * P : (i + 1) * P].rearrange("p j (c n) -> p c j n", n=LINE),
                                  ACT.Copy)

from contextlib import ExitStack

import concourse.mybir as mybir
from concourse.masks import make_identity

N, T, D, DV, NQ = 512, 1024, 512, 128, 256
CAP = 2.0
FLOPS = 2 * NQ * N * D + 2 * NQ * N * DV

F32 = mybir.dt.float32
BF16 = mybir.dt.bfloat16
I32 = mybir.dt.int32
U32 = mybir.dt.uint32
U16 = mybir.dt.uint16
U8 = mybir.dt.uint8
FP8X4 = mybir.dt.float8_e4m3fn_x4
ACT = mybir.ActivationFunctionType
ALU = mybir.AluOpType

P = 128
PACK = 4
QT = NQ // P
H = N // 2
PER_COLUMN = 16
QUADRANT = 32
LINE = 4
VS_ROW = 16
FIRST = 2 * NQ + P
PREFIX = T - (N - H)


def tile_attend_soft_cap_gate_srtq256n512t1024_kernel(tc, qT, k_words, k_scales, vT, vs, og, offs, out):
    nc = tc.nc
    with ExitStack() as ctx:
        sb = ctx.enter_context(tc.tile_pool(name="sb", bufs=1))
        ps = ctx.enter_context(tc.psum_pool(name="ps", bufs=1))

        def tile(name, shape, dtype, tag=None):
            return sb.tile(shape, dtype, name=name, tag=tag or name, align_bytes=64)

        def quantise(codes, scales, grouped):
            nc.vector.quantize_mx(codes.bitcast(FP8X4), scales, grouped.rearrange("p c j -> p (c j)"))

        def entries(first, last):
            return offsets[:, first // PER_COLUMN : last // PER_COLUMN]

        offsets = sb.tile([P, N // PER_COLUMN], U16, name="offsets")
        nc.sync.dma_start(offsets[:], offs)
        kw_pool = tile("kw_pool", [P, T], I32)
        kw_rows = k_words[0].rearrange("p n t -> p (n t)").bitcast(I32)
        q_rows = qT[0].rearrange("(p j) q -> p (j q)", j=PACK)
        q_raw = tile("q_raw", [P, PACK, NQ], F32)
        q_flat = q_raw[:].rearrange("p j q -> p (j q)")
        nc.scalar.dma_start(q_flat[:, 0:FIRST], q_rows[:, 0:FIRST])
        ks_pool = tile("ks_pool", [P, T], U8)
        nc.vector.memset(ks_pool[:].bitcast(I32), 0)
        for r in range(PACK):
            queue = nc.scalar if r % 2 else nc.sync
            queue.dma_start(ks_pool[r:P:QUADRANT, :].bitcast(I32), k_scales[0, r : D // 32 : PACK, :].bitcast(I32))
        ident = tile("ident", [P, P], F32)
        nc.vector.memset(ident[:], 0.0)
        vs_pool = tile("vs_pool", [P, T], F32)
        nc.vector.memset(vs_pool[:].bitcast(I32), 0)
        nc.sync.dma_start(q_flat[:, FIRST : PACK * NQ], q_rows[:, FIRST : PACK * NQ])
        nc.sync.dma_start(kw_pool[:, 0:PREFIX], kw_rows[:, 0:PREFIX])
        nc.sync.dma_start(kw_pool[:, PREFIX:T], kw_rows[:, PREFIX:T])
        nc.sync.dma_start(vs_pool[VS_ROW : VS_ROW + 1, :], vs[0:1, :])
        v_pool = tile("v_pool", [P, T], F32)
        nc.sync.dma_start(v_pool[:], vT)
        og_sb = tile("og_sb", [P, QT, DV], F32)
        nc.sync.dma_start(og_sb[:], og[0].rearrange("(i p) e -> p i e", p=P))

        make_identity(nc, ident[:], nomemset=True)

        q_bf = [tile(f"q_bf{i}", [P, P, PACK], BF16) for i in range(QT)]
        for i, first, last in ((0, 0, 3), (0, 3, PACK), (1, 0, PACK)):
            nc.scalar.activation(q_bf[i][:, :, first:last].rearrange("p (c n) j -> p c j n", n=LINE),
                                 q_raw[:, first:last, i * P : (i + 1) * P].rearrange("p j (c n) -> p c j n", n=LINE),
                                 ACT.Copy)
        q_codes = [tile(f"q_codes{i}", [P, P], U32) for i in range(QT)]
        q_scales = [tile(f"q_scales{i}", [P, P], U8) for i in range(QT)]

        kw_g = [tile("kw_g0", [P, H], U32), tile("kw_g1", [P, H], U32)]
        ks_g = tile("ks_g", [P, N], U8)
        nc.vector.tensor_copy(ks_g[:], ks_pool[:].indirect(offsets[:]))
        quantise(q_codes[0][:], q_scales[0][:], q_bf[0][:])
        nc.vector.tensor_copy(kw_g[0][:], kw_pool[:, 0:PREFIX].bitcast(U32).indirect(entries(0, H)))
        nc.vector.tensor_copy(kw_g[1][:], kw_pool[:].bitcast(U32).indirect(entries(H, N)))
        quantise(q_codes[1][:], q_scales[1][:], q_bf[1][:])
        vs_g = tile("vs_g", [P, N], F32, tag="q_raw")
        nc.scalar.activation(vs_g[:], vs_pool[:].indirect(offsets[:]), ACT.Copy)
        v_words = tile("v_words", [P, H], F32)
        nc.vector.tensor_copy(v_words[:].bitcast(BF16), v_pool[:].indirect(offsets[:]))

        th_both = tile("th_both", [P, QT * N], F32, tag="vs_pool")
        th = [th_both[:, i * N : (i + 1) * N].rearrange("p (t s) -> p t s", t=PACK) for i in range(QT)]
        for i in range(QT):
            for h in range(2):
                score = ps.tile([P, H], F32, name=f"score{i}{h}", tag=f"score{i}{h}")
                nc.tensor.matmul_mx(score[:], lhsT=q_codes[i][:].bitcast(FP8X4), lhsT_scale=q_scales[i][:],
                                    rhs=kw_g[h][:].bitcast(FP8X4), rhs_scale=ks_g[:, h * H : (h + 1) * H],
                                    start=True, stop=True)
                nc.scalar.activation(th[i][:, :, h * H // PACK : (h + 1) * H // PACK],
                                     score[:].rearrange("p (s t) -> p t s", t=PACK), ACT.Tanh, scale=1.0 / CAP)

        vs_col = tile("vs_col", [P, PACK], F32)
        nc.sync.dma_start(vs_col[:], vs_g[VS_ROW : VS_ROW + 1, :])
        v_t = ps.tile([P, 2, DV], F32, name="v_t")
        for u in range(2):
            nc.tensor.transpose(v_t[:, u, :], v_words[:, u:H:2], ident[:])

        total = tile("total", [P, QT], F32)
        parts = tile("parts", [P, QT, 2], F32)
        p = []
        for i in range(QT):
            neg_c = tile(f"neg_c{i}", [P, N], F32)
            neg_m = tile(f"neg_m{i}", [P, 1], F32)
            nc.vector.tensor_scalar(neg_c[:], th_both[:, i * N : (i + 1) * N], -CAP, None, ALU.mult, ALU.min,
                                    accum_out=neg_m[:])
            p.append(tile(f"p{i}", [P, N], F32))
            for h in range(2):
                places = slice(h * H, (h + 1) * H)
                nc.scalar.activation(p[i][:, places], neg_c[:, places], ACT.Exp, bias=neg_m[:], scale=-1.0,
                                     accum_out=parts[:, i, h : h + 1])
        v_bf = tile("v_bf", [P, DV, PACK], BF16, tag="vs_pool")
        nc.vector.tensor_copy(v_bf[:].bitcast(F32), v_t[:].rearrange("p u e -> p e u"))
        for i in range(QT):
            nc.scalar.activation(total[:, i : i + 1], parts[:, i, 0:1], ACT.Identity, bias=parts[:, i, 1:2])

        w_bf = [tile(f"w_bf{i}", [P, P, PACK], BF16) for i in range(QT)]
        for i in range(QT):
            p_t = ps.tile([P, PACK, P], F32, name=f"p_t{i}")
            for t in range(PACK):
                nc.tensor.transpose(p_t[:, t, :], p[i][:, t * P : (t + 1) * P], ident[:])
            width = P // 2 if i == QT - 1 else P
            for first in range(0, P, width):
                nc.vector.tensor_tensor(w_bf[i][:, first : first + width, :],
                                        p_t[:, :, first : first + width].rearrange("p t q -> p q t"),
                                        vs_col[:].unsqueeze(1).to_broadcast([P, width, PACK]), ALU.mult)

        v_codes = tile("v_codes", [P, DV], U32)
        v_scales = tile("v_scales", [P, DV], U8)
        w_codes = [tile(f"w_codes{i}", [P, P], U32) for i in range(QT)]
        w_scales = [tile(f"w_scales{i}", [P, P], U8) for i in range(QT)]
        quantise(w_codes[0][:], w_scales[0][:], w_bf[0][:])
        quantise(v_codes[:], v_scales[:], v_bf[:])
        for first in range(0, P, P // 2):
            columns = slice(first, first + P // 2)
            quantise(w_codes[1][:, columns], w_scales[1][:, columns], w_bf[1][:, columns, :])

        gate_th = tile("gate_th", [P, QT, DV], F32, tag="parts")
        nc.scalar.activation(gate_th[:], og_sb[:], ACT.Tanh, scale=0.5)
        gate = tile("gate", [P, QT, DV], F32)
        nc.scalar.activation(gate[:], gate_th[:], ACT.Copy, scale=0.5, bias=0.5)
        inv = tile("inv", [P, QT], F32)
        nc.vector.reciprocal(inv[:], total[:])

        for i in range(QT):
            y = ps.tile([P, DV], F32, name=f"y{i}", tag=f"score0{i}")
            nc.tensor.matmul_mx(y[:], lhsT=w_codes[i][:].bitcast(FP8X4), lhsT_scale=w_scales[i][:],
                                rhs=v_codes[:].bitcast(FP8X4), rhs_scale=v_scales[:], start=True, stop=True)
            res = tile(f"res{i}", [P, DV], F32)
            nc.vector.scalar_tensor_tensor(res[:], y[:], inv[:, i : i + 1], gate[:, i, :], ALU.mult, ALU.mult)
            (nc.sync if i == QT - 1 else nc.scalar).dma_start(out[0, i * P : (i + 1) * P, :], res[:])
